import numpy as np
import ml_dtypes


def mxq(x, axis, fmt="e4m3"):
    dtype, down = {"e4m3": (ml_dtypes.float8_e4m3fn, 7), "e5m2": (ml_dtypes.float8_e5m2, 14)}[fmt]
    v = np.moveaxis(np.asarray(x, np.float32).astype(ml_dtypes.bfloat16).astype(np.float64), axis, -1)
    blocks = v.reshape(v.shape[:-1] + (-1, 32))
    amax = np.abs(blocks).max(-1, keepdims=True)
    byte = np.maximum(np.where(amax > 0, np.frexp(amax)[1] - 1 + 127, 0) - down, 1)
    scale = np.exp2(byte - 127.0)
    codes = (blocks / scale).astype(np.float32).astype(dtype).astype(np.float64)
    return np.moveaxis((codes * scale).reshape(v.shape), -1, axis)


WIDE = False


def mx_kscale(k):
    if not WIDE:
        return np.ones(k)
    levels = np.array([30, -30])
    if k % 512:
        return np.exp2(np.random.permutation(np.resize(levels, k // 32))).repeat(32)
    a = np.empty((k // 512, 16))
    for p in range(k // 512):
        a[p, :8] = np.random.permutation(np.resize(levels, 8))
        for g in range(8):
            far = levels[np.abs(levels - a[p, g]) >= 10]
            a[p, g + 8] = far[np.random.randint(len(far))]
    return np.exp2(a.ravel()).repeat(32)


BF16 = ml_dtypes.bfloat16


def bf(x):
    return np.asarray(x, np.float32).astype(BF16)


def f64(x):
    return np.asarray(x).astype(np.float64)


E2M1 = np.array([0.0, 0.5, 1.0, 1.5, 2.0, 3.0, 4.0, 6.0, -0.0, -0.5, -1.0, -1.5, -2.0, -3.0, -4.0, -6.0])


def pack_weight(w, fmt):
    k, n = w.shape
    w = f64(bf(w)).reshape(k // 32, 32, n)
    amax = np.abs(w).max(1)
    if fmt == "e4m3":
        byte = np.frexp(amax)[1] - 1 + 127 - 7
    else:
        mant, ex = np.frexp(amax / 6.0)
        byte = np.where(mant > 0.5, ex, ex - 1) + 127
    byte = np.clip(np.where(amax > 0, byte, 1), 1, 254)
    scaled = (w * np.exp2(127.0 - byte)[:, None, :]).reshape(k, n).astype(np.float32)
    by_word = np.ascontiguousarray(scaled.reshape(k // 512, 128, 4, n).transpose(0, 1, 3, 2))
    if fmt == "e4m3":
        words = by_word.astype(ml_dtypes.float8_e4m3fn).view(np.uint8)
    else:
        c = by_word.astype(ml_dtypes.float4_e2m1fn).view(np.uint8) & 0xF
        words = c[..., 0::2] | (c[..., 1::2] << 4)
    return np.ascontiguousarray(words), np.ascontiguousarray(byte.astype(np.uint8).reshape(k // 512, 16, n))


def unpack_weight(words, scales, fmt):
    g, p, n, _ = words.shape
    if fmt == "e4m3":
        vals = np.ascontiguousarray(words).view(ml_dtypes.float8_e4m3fn).astype(np.float64)
    else:
        nib = np.empty((g, p, n, 4), np.uint8)
        nib[..., 0::2] = words & 0xF
        nib[..., 1::2] = words >> 4
        vals = E2M1[nib]
    vals = vals * np.repeat(np.exp2(scales.astype(np.float64) - 127.0), 8, axis=1)[..., None]
    return vals.transpose(0, 1, 3, 2).reshape(g * 512, n)
def pack4(w):
    words, scales = pack_weight(w, "e2m1")
    return words.reshape(words.shape[0], 128, -1), scales


def unpack4(words, scales):
    return unpack_weight(words.reshape(words.shape[0], 128, -1, 2), scales, "e2m1")


M, R, T, N, B = 1024, 1024, 2048, 1024, 4


def setup_inputs():
    s, t = mx_kscale(R), mx_kscale(T)
    filters = np.random.standard_normal((R, M)) * s[:, None]
    channel = np.random.standard_normal((R, T)) / np.sqrt(R) / s[:, None] * t
    precoders = np.random.standard_normal((T, N)) / np.sqrt(T) / t[:, None]
    h_words, h_scales = pack4(channel)
    return {"u": bf(filters),
            "h_words": h_words,
            "h_scales": h_scales,
            "gain": bf(1 + 0.1 * np.random.standard_normal(T)),
            "v": bf(precoders),
            "power": bf(np.random.uniform(0.5, 1.5, N) / B)}


def reference(u, h_words, h_scales, gain, v, power):
    seen = mxq(f64(u), 0, "e4m3").T @ unpack4(h_words, h_scales)
    seen = seen * f64(gain)
    f = mxq(seen, 1, "e5m2") @ mxq(f64(v), 0, "e4m3")
    weighted = f ** 2 * f64(power)
    leak = weighted.reshape(M // B, B, N // B, B).sum(axis=(1, 3))
    return f, leak

@@ -1,0 +1,356 @@
+from contextlib import ExitStack
+
+import concourse.mybir as mybir
+from concourse.masks import make_identity
+
+R, M, T, N = 1024, 1024, 2048, 1024
+B = 4
+
+FLOPS = 2 * R * M * T + 2 * M * T * N + 4 * M * N
+
+F32 = mybir.dt.float32
+BF16 = mybir.dt.bfloat16
+I32 = mybir.dt.int32
+U32 = mybir.dt.uint32
+U8 = mybir.dt.uint8
+E4M3 = mybir.dt.float8_e4m3fn_x4
+E5M2 = mybir.dt.float8_e5m2_x4
+E2M1 = mybir.dt.float4_e2m1fn_x4
+ADD = mybir.AluOpType.add
+MULT = mybir.AluOpType.mult
+ACTF = mybir.ActivationFunctionType
+
+P = 128
+KG = 2
+TG = 4
+HALF = 512
+NH = 512
+
+
+def tile_interference_alignment_leakage_s9_kernel(tc, u, h_words, h_scales, gain, v, power, out_0, out_1):
+    nc = tc.nc
+    with ExitStack() as ctx:
+        keep = ctx.enter_context(tc.tile_pool(name="keep", bufs=1))
+        stage = ctx.enter_context(tc.tile_pool(name="stage", bufs=2))
+        psum = ctx.enter_context(tc.psum_pool(name="psum", bufs=1))
+
+        h_raw = keep.tile([P, KG, 2 * T], U8, align_bytes=64)
+        h_codes = keep.tile([P, KG, TG, 1024], U8, align_bytes=64)
+        hs_raw = keep.tile([P, KG, T], U8, align_bytes=64)
+        h_scale = keep.tile([P, KG, TG, 512], U8, align_bytes=64)
+        u_codes = keep.tile([P, 2, KG, HALF], U32, align_bytes=64)
+        u_scale = keep.tile([P, 2, KG, HALF], U8, align_bytes=64)
+        v_codes = keep.tile([P, TG, 2, NH], U32, align_bytes=64)
+        v_scale = keep.tile([P, TG, 2, NH], U8, align_bytes=64)
+        g_codes = keep.tile([P, 2, TG, HALF], U32, align_bytes=64)
+        g_scale = keep.tile([P, 2, TG, HALF], U8, align_bytes=64)
+        f_sb = keep.tile([P, 2, B, N], F32, align_bytes=64)
+        gain_rows = keep.tile([P, P], BF16, align_bytes=64)
+        gain_cols = keep.tile([P, 16], F32, align_bytes=64)
+        ident = keep.tile([P, P], BF16, align_bytes=64)
+        pw = keep.tile([P, N], BF16, align_bytes=64)
+        warm = keep.tile([P, 2], F32, align_bytes=64)
+        u_raw = {(h, k): keep.tile([P, 4, HALF], BF16, align_bytes=64, name="u_raw%d%d" % (h, k)) for h in range(2) for k in range(KG)}
+        v_raw = {g: keep.tile([P, 4, N], BF16, align_bytes=64, name="v_raw%d" % g) for g in range(TG)}
+
+        def load_u(h, k):
+            nc.sync.dma_start(
+                out=u_raw[h, k][:],
+                in_=u[512 * k : 512 * k + 512, HALF * h : HALF * h + HALF].rearrange("(p j) w -> p j w", j=4),
+            )
+
+        def load_h(first, groups):
+            cols = slice(1024 * first, 1024 * (first + groups))
+            nc.sync.dma_start(out=h_raw[:, :, cols].bitcast(I32), in_=h_words.rearrange("g p b -> p g b")[:, :, cols].bitcast(I32))
+
+        def load_v(g):
+            rows = v[512 * g : 512 * g + 512, :].rearrange("(a t r) n -> r a t n", t=4, r=4)
+            for r in range(4):
+                nc.sync.dma_start(out=v_raw[g][r:P:4, :, :], in_=rows[r])
+
+        nc.vector.memset(warm[:], 0.0)
+        nc.scalar.activation(out=warm[:, 0:1], in_=warm[:, 1:2], func=ACTF.Square)
+        nc.gpsimd.memset(hs_raw[:].rearrange("p g b -> p (g b)").bitcast(I32), 0)
+        nc.gpsimd.memset(gain_rows[:], 0.0)
+        make_identity(nc, ident[:])
+        load_h(0, 1)
+        load_u(0, 0)
+        load_u(0, 1)
+        for q in range(4):
+            nc.scalar.dma_start(
+                out=hs_raw[32 * q : 32 * q + 4, :, :].bitcast(I32),
+                in_=h_scales[:, 4 * q : 4 * q + 4, :].rearrange("g q b -> q g b").bitcast(I32),
+            )
+        for g in range(TG):
+            nc.gpsimd.dma_start(
+                out=gain_rows[4 * g : 4 * g + 4, :].rearrange("t (a r) -> t a r", r=4),
+                in_=gain[512 * g : 512 * g + 512].rearrange("(a t r) -> t a r", t=4, r=4),
+            )
+
+        load_u(1, 0)
+        load_h(1, 1)
+        load_u(1, 1)
+        load_v(0)
+        load_h(2, 2)
+        load_v(1)
+        load_v(2)
+        load_v(3)
+        nc.sync.dma_start(out=pw[:], in_=power.partition_broadcast(P))
+
+        def interleave(engine, out, in_):
+            o = out.rearrange("p (c i t) -> p c t i", i=4, t=4)
+            s = in_.rearrange("p t (c i) -> p c t i", i=4)
+            if engine == "v":
+                nc.vector.tensor_copy(out=o, in_=s)
+            else:
+                nc.scalar.copy(out=o, in_=s)
+
+        u_group = {}
+
+        def u_inter(h, k, part, engine):
+            if (h, k) not in u_group:
+                u_group[h, k] = stage.tile([P, 4 * HALF], BF16, align_bytes=64, name="u_grp", bufs=4)
+            interleave(engine, u_group[h, k][:, 1024 * part : 1024 * part + 1024], u_raw[h, k][:, :, 256 * part : 256 * part + 256])
+
+        def u_quant(h, k, part):
+            cols = slice(256 * part, 256 * part + 256)
+            nc.vector.quantize_mx(
+                out=u_codes[:, h, k, cols].bitcast(E4M3), scales=u_scale[:, h, k, cols],
+                in_=u_group[h, k][:, 1024 * part : 1024 * part + 1024],
+            )
+
+        v_group = {}
+
+        def v_inter(g, n, engine, part, parts):
+            if (g, n) not in v_group:
+                v_group[g, n] = stage.tile([P, 4 * NH], BF16, align_bytes=64, name="v_grp", bufs=4)
+            w = NH // parts
+            lo = w * part
+            interleave(engine, v_group[g, n][:, 4 * lo : 4 * lo + 4 * w], v_raw[g][:, :, NH * n + lo : NH * n + lo + w])
+
+        def v_quant(g, n):
+            nc.vector.quantize_mx(
+                out=v_codes[:, g, n, :].bitcast(E4M3), scales=v_scale[:, g, n, :], in_=v_group[g, n][:],
+            )
+
+        def h_permute(g):
+            for k in range(KG):
+                nc.vector.tensor_copy(
+                    out=h_codes[:, k, g, :].bitcast(I32).rearrange("p (t a w) -> p t a w", t=4, w=2),
+                    in_=h_raw[:, k, 1024 * g : 1024 * g + 1024].bitcast(I32).rearrange("p (a t w) -> p t a w", t=4, w=2),
+                )
+
+        def h_scale_permute(k):
+            nc.vector.tensor_copy(
+                out=h_scale[:, k, :, :].rearrange("p g b -> p (g b)").bitcast(I32).rearrange("p (g t a) -> p g t a", g=4, t=4),
+                in_=hs_raw[:, k, :].bitcast(I32).rearrange("p (g a t) -> p g t a", g=4, t=4),
+            )
+
+        s1_bank = {}
+
+        def s1(h, g, b):
+            bank = psum.tile([P, 4, P], F32, name="bank%d" % ((16 * h + 4 * g + b) % 3))
+            s1_bank[h, g, b] = bank
+            cols = slice(P * b, P * b + P)
+            for t in range(4):
+                for k in range(KG):
+                    nc.tensor.matmul_mx(
+                        out=bank[:, t, :],
+                        lhsT=h_codes[:, k, g, 256 * t : 256 * t + 256].bitcast(E2M1),
+                        lhsT_scale=h_scale[:, k, g, P * t : P * t + P],
+                        rhs=u_codes[:, h, k, cols].bitcast(E4M3),
+                        rhs_scale=u_scale[:, h, k, cols],
+                        start=(k == 0), stop=(k == KG - 1),
+                    )
+
+        g_group = {}
+
+        def g_copy(h, g, b):
+            if b == 0:
+                g_group[h, g] = stage.tile([P, B, P, 4], BF16, align_bytes=64, name="g_grp", bufs=2)
+            nc.vector.tensor_tensor(
+                out=g_group[h, g][:, :, 32 * b : 32 * b + 32, :],
+                in0=s1_bank[h, g, b][:].rearrange("p t (i a) -> p a i t", a=B),
+                in1=gain_cols[:, 4 * g : 4 * g + 4].unsqueeze(1).unsqueeze(1).to_broadcast([P, B, 32, 4]),
+                op=MULT,
+            )
+
+        def g_quant(h, g):
+            nc.vector.quantize_mx(
+                out=g_codes[:, h, g, :].bitcast(E5M2), scales=g_scale[:, h, g, :],
+                in_=g_group[h, g][:].rearrange("p a i t -> p (a i t)"),
+            )
+
+        s2_bank = {}
+        BANKS = {(0, 0): (3, 4, 5, 6), (0, 1): (7, 3, 4, 5), (1, 0): (6, 7, 3, 4), (1, 1): (5, 0, 1, 2)}
+
+        def s2(h, n, a, g):
+            if g == 0:
+                s2_bank[h, n, a] = psum.tile([P, NH], F32, name="bank%d" % BANKS[h, n][a])
+            cols = slice(P * a, P * a + P)
+            nc.tensor.matmul_mx(
+                out=s2_bank[h, n, a][:],
+                lhsT=g_codes[:, h, g, cols].bitcast(E5M2),
+                lhsT_scale=g_scale[:, h, g, cols],
+                rhs=v_codes[:, g, n, :].bitcast(E4M3),
+                rhs_scale=v_scale[:, g, n, :],
+                start=(g == 0), stop=(g == TG - 1),
+            )
+
+        squares = {}
+
+        def f_copy(h, n, a, engine="s"):
+            bank = s2_bank[h, n, a]
+            dst = f_sb[:, h, a, NH * n : NH * n + NH]
+            if engine == "s":
+                nc.scalar.copy(out=dst, in_=bank[:])
+            else:
+                nc.vector.tensor_copy(out=dst, in_=bank[:])
+            rows = out_0[HALF * h : HALF * h + HALF, NH * n : NH * n + NH].rearrange("(i a) n -> i a n", a=B)
+            nc.sync.dma_start(out=rows[:, a, :], in_=dst)
+
+        def f_square(h, n, a, psum=False, parts=1, part=0):
+            if a == 0:
+                squares[h, n] = stage.tile([P, B, NH], F32, align_bytes=64, name="sq", bufs=2)
+            w = NH // parts
+            lo = w * part
+            src = s2_bank[h, n, a][:, lo : lo + w] if psum else f_sb[:, h, a, NH * n + lo : NH * n + lo + w]
+            nc.scalar.activation(out=squares[h, n][:, a, lo : lo + w], in_=src, func=ACTF.Square)
+
+        total = {}
+
+        def leak_add(h, n, a, parts=1, part=0):
+            if a == 1 and part == 0:
+                total[h, n] = stage.tile([P, NH], F32, align_bytes=64, name="total", bufs=3)
+            w = NH // parts
+            cols = slice(w * part, w * part + w)
+            nc.vector.tensor_tensor(
+                out=total[h, n][:, cols],
+                in0=squares[h, n][:, 0, cols] if a == 1 else total[h, n][:, cols],
+                in1=squares[h, n][:, a, cols], op=ADD,
+            )
+
+        def leak_weigh(h, n, parts=1, part=0):
+            w = NH // parts
+            lo = w * part
+            nc.vector.tensor_tensor(
+                out=total[h, n][:, lo : lo + w], in0=total[h, n][:, lo : lo + w], in1=pw[:, NH * n + lo : NH * n + lo + w], op=MULT,
+            )
+
+        leak_sb = {}
+
+        def leak_sum(h, n, parts=1, part=0):
+            if part == 0:
+                leak_sb[h, n] = stage.tile([P, P], F32, align_bytes=64, name="leak", bufs=2)
+            w = NH // parts
+            nc.vector.tensor_reduce(
+                out=leak_sb[h, n][:, w * part // B : w * (part + 1) // B],
+                in_=total[h, n][:, w * part : w * part + w].rearrange("p (j b) -> p j b", b=B), axis=mybir.AxisListType.X, op=ADD,
+            )
+            if part == parts - 1:
+                nc.sync.dma_start(out=out_1[P * h : P * h + P, P * n : P * n + P], in_=leak_sb[h, n][:])
+
+        todo = {}
+
+        def at(slot, fn, *args):
+            todo.setdefault(slot, []).append((fn, args))
+
+        def order():
+            h_scale_permute(0)
+            h_scale_permute(1)
+            h_permute(0)
+            u_inter(0, 0, 0, "v")
+            u_inter(0, 0, 1, "s")
+            u_quant(0, 0, 0)
+            u_inter(0, 1, 0, "v")
+            u_inter(0, 1, 1, "s")
+            gain_ps = psum.tile([P, P], BF16, name="bank7")
+            nc.tensor.transpose(gain_ps[:], gain_rows[:], ident[:])
+            u_quant(0, 1, 0)
+            nc.vector.tensor_copy(out=gain_cols[:], in_=gain_ps[:, 0:16])
+
+            at(0, u_quant, 0, 0, 1)
+            at(0, u_quant, 0, 1, 1)
+            for g in range(1, TG):
+                at(4 * g - 2, h_permute, g)
+            for k in range(KG):
+                for part in range(2):
+                    at(0, u_inter, 1, k, part, "s")
+                    at(6 + 4 * k + part, u_quant, 1, k, part)
+            for g in range(TG):
+                at(1, v_inter, g, 0, "s", 0, 1)
+                at(9 + 3 * g, v_quant, g, 0)
+            for g in range(3):
+                at(12, v_inter, g, 1, "s", 0, 1)
+                at(17 + 3 * g, v_quant, g, 1)
+            at(18, v_inter, 3, 1, "v", 0, 2)
+            at(20, v_inter, 3, 1, "v", 1, 2)
+            at(22, v_quant, 3, 1)
+            for a in range(B):
+                for g in range(TG):
+                    at(3 * g + 11 + a, s2, 0, 0, a, g)
+                    at(24 + a, s2, 0, 1, a, g)
+                    at(28 + a if g < 3 else 34, s2, 1, 0, a, g)
+                    at(39 + a, s2, 1, 1, a, g)
+            for a in range(B):
+                at(21 + a, f_copy, 0, 0, a)
+                at(24 + a, f_square, 0, 0, a)
+                at(25 + a, f_copy, 0, 1, a, "s")
+                at(27 + a, f_square, 0, 1, a)
+                at(36 + a, f_copy, 1, 0, a, "s" if a % 2 else "s")
+                at(36 + a, f_square, 1, 0, a)
+            for i in range(3):
+                at(28 + i, leak_add, 0, 0, i + 1)
+                at(33 + i, leak_add, 0, 1, i + 1)
+            at(31, leak_weigh, 0, 0)
+            at(32, leak_sum, 0, 0)
+            at(36, leak_weigh, 0, 1)
+            at(37, leak_sum, 0, 1)
+            at(40, f_copy, 1, 1, 0, "v")
+            at(40, f_square, 1, 1, 0)
+            at(40, leak_add, 1, 0, 1)
+            at(41, f_copy, 1, 1, 1, "v")
+            at(41, f_square, 1, 1, 1)
+            at(42, leak_add, 1, 0, 2)
+            at(42, leak_add, 1, 0, 3)
+            at(43, f_copy, 1, 1, 2, "v")
+            at(43, leak_weigh, 1, 0)
+            at(43, f_square, 1, 1, 2)
+            at(44, leak_add, 1, 1, 1)
+            at(44, leak_sum, 1, 0)
+            at(44, leak_add, 1, 1, 2)
+            for part in range(2):
+                at(44, f_square, 1, 1, 3, True, 2, part)
+            at(44, f_copy, 1, 1, 3, "s")
+            for part in range(2):
+                at(44, leak_add, 1, 1, 3, 2, part)
+            for part in range(2):
+                at(45, leak_weigh, 1, 1, 2, part)
+            for part in range(2):
+                at(46, leak_sum, 1, 1, 2, part)
+
+            def name(s):
+                return s // 16, (s // 4) % 4, s % 4
+
+            s1(*name(0))
+            s1(*name(1))
+            for s in range(max(todo) + 1):
+                if s < 32:
+                    g_copy(*name(s))
+                if 4 <= s <= 32 and s % 4 == 0:
+                    g_quant(*name(s - 1)[:2])
+                if s < 32:
+                    for fn, args in todo.get(s, ()):
+                        if fn is not s2:
+                            fn(*args)
+                    if s + 2 < 32:
+                        s1(*name(s + 2))
+                    for fn, args in todo.get(s, ()):
+                        if fn is s2:
+                            fn(*args)
+                else:
+                    for fn, args in todo.get(s, ()):
+                        fn(*args)
+
+        with tc.manual_schedule():
+            order()

@@ -18,13 +18,18 @@ E5M2 = mybir.dt.float8_e5m2_x4
 E2M1 = mybir.dt.float4_e2m1fn_x4
 ADD = mybir.AluOpType.add
 MULT = mybir.AluOpType.mult
-ACTF = mybir.ActivationFunctionType
+SQUARE = mybir.ActivationFunctionType.Square
 
 P = 128
-KG = 2
-TG = 4
-HALF = 512
-NH = 512
+PACK = 4
+PASS = P * PACK
+KP = R // PASS
+TG = T // PASS
+HALF = M // 2
+BLOCKS = HALF // P
+SETS = P // B
+NH = N // 2
+QUARTER = 256
 
 
 def tile_interference_alignment_leakage_s9_kernel(tc, u, h_words, h_scales, gain, v, power, out_0, out_1):
@@ -33,160 +38,152 @@ def tile_interference_alignment_leakage_s9_kernel(tc, u, h_words, h_scales, gain
         keep = ctx.enter_context(tc.tile_pool(name="keep", bufs=1))
         stage = ctx.enter_context(tc.tile_pool(name="stage", bufs=2))
         psum = ctx.enter_context(tc.psum_pool(name="psum", bufs=1))
+        ctx.enter_context(tc.manual_schedule())
 
-        h_raw = keep.tile([P, KG, 2 * T], U8, align_bytes=64)
-        h_codes = keep.tile([P, KG, TG, 1024], U8, align_bytes=64)
-        hs_raw = keep.tile([P, KG, T], U8, align_bytes=64)
-        h_scale = keep.tile([P, KG, TG, 512], U8, align_bytes=64)
-        u_codes = keep.tile([P, 2, KG, HALF], U32, align_bytes=64)
-        u_scale = keep.tile([P, 2, KG, HALF], U8, align_bytes=64)
-        v_codes = keep.tile([P, TG, 2, NH], U32, align_bytes=64)
-        v_scale = keep.tile([P, TG, 2, NH], U8, align_bytes=64)
-        g_codes = keep.tile([P, 2, TG, HALF], U32, align_bytes=64)
-        g_scale = keep.tile([P, 2, TG, HALF], U8, align_bytes=64)
-        f_sb = keep.tile([P, 2, B, N], F32, align_bytes=64)
-        gain_rows = keep.tile([P, P], BF16, align_bytes=64)
-        gain_cols = keep.tile([P, 16], F32, align_bytes=64)
-        ident = keep.tile([P, P], BF16, align_bytes=64)
-        pw = keep.tile([P, N], BF16, align_bytes=64)
-        warm = keep.tile([P, 2], F32, align_bytes=64)
-        u_raw = {(h, k): keep.tile([P, 4, HALF], BF16, align_bytes=64, name="u_raw%d%d" % (h, k)) for h in range(2) for k in range(KG)}
-        v_raw = {g: keep.tile([P, 4, N], BF16, align_bytes=64, name="v_raw%d" % g) for g in range(TG)}
+        def sbuf(shape, dtype, name):
+            return keep.tile(shape, dtype, align_bytes=64, name=name)
 
-        def load_u(h, k):
+        def bank(index, shape, dtype):
+            return psum.tile(shape, dtype, name="bank%d" % index)
+
+        u_raw = {(h, k, c): sbuf([P, PACK, QUARTER], BF16, "u_raw%d%d%d" % (h, k, c)) for h in range(2) for k in range(KP) for c in range(2)}
+        u_codes = sbuf([P, 2, KP, HALF], U32, "u_codes")
+        u_scale = sbuf([P, 2, KP, HALF], U8, "u_scale")
+        h_raw = [sbuf([P, KP, 2 * PASS], U8, "h_raw%d" % g) for g in range(TG)]
+        h_codes = sbuf([P, KP, TG, 2 * PASS], U8, "h_codes")
+        hs_raw = sbuf([P, KP, T], U8, "hs_raw")
+        h_scale = sbuf([P, KP, TG, PASS], U8, "h_scale")
+        v_raw = [sbuf([P, PACK, N], BF16, "v_raw%d" % g) for g in range(TG)]
+        v_codes = sbuf([P, TG, 2, NH], U32, "v_codes")
+        v_scale = sbuf([P, TG, 2, NH], U8, "v_scale")
+        g_codes = sbuf([P, 2, TG, HALF], U32, "g_codes")
+        g_scale = sbuf([P, 2, TG, HALF], U8, "g_scale")
+        f_sb = sbuf([P, 2, B, N], F32, "f_sb")
+        power_sb = sbuf([P, N], BF16, "power_sb")
+        gain_rows = sbuf([P, P], BF16, "gain_rows")
+        gain_cols = sbuf([P, TG * PACK], F32, "gain_cols")
+        ident = sbuf([P, P], BF16, "ident")
+        zeros = sbuf([P, 512], BF16, "zeros")
+        one_column = sbuf([P, 2], F32, "one_column")
+
+
+        def load_u(h, k, c):
+            lo = HALF * h + QUARTER * c
             nc.sync.dma_start(
-                out=u_raw[h, k][:],
-                in_=u[512 * k : 512 * k + 512, HALF * h : HALF * h + HALF].rearrange("(p j) w -> p j w", j=4),
+                out=u_raw[h, k, c][:],
+                in_=u[PASS * k : PASS * k + PASS, lo : lo + QUARTER].rearrange("(p t) w -> p t w", t=PACK),
             )
 
-        def load_h(first, groups):
-            cols = slice(1024 * first, 1024 * (first + groups))
-            nc.sync.dma_start(out=h_raw[:, :, cols].bitcast(I32), in_=h_words.rearrange("g p b -> p g b")[:, :, cols].bitcast(I32))
+        def load_h(g):
+            words = h_words.rearrange("k p b -> p k b")[:, :, 2 * PASS * g : 2 * PASS * g + 2 * PASS]
+            nc.sync.dma_start(out=h_raw[g][:].bitcast(I32), in_=words.bitcast(I32))
+
+        def load_h_scales(q):
+            nc.sync.dma_start(
+                out=hs_raw[32 * q : 32 * q + 4, :, :].bitcast(I32),
+                in_=h_scales[:, 4 * q : 4 * q + 4, :].rearrange("k q n -> q k n").bitcast(I32),
+            )
 
         def load_v(g):
-            rows = v[512 * g : 512 * g + 512, :].rearrange("(a t r) n -> r a t n", t=4, r=4)
+            rows = v[PASS * g : PASS * g + PASS, :].rearrange("(a t r) n -> r a t n", t=PACK, r=4)
             for r in range(4):
                 nc.sync.dma_start(out=v_raw[g][r:P:4, :, :], in_=rows[r])
 
-        nc.vector.memset(warm[:], 0.0)
-        nc.scalar.activation(out=warm[:, 0:1], in_=warm[:, 1:2], func=ACTF.Square)
-        nc.gpsimd.memset(hs_raw[:].rearrange("p g b -> p (g b)").bitcast(I32), 0)
-        nc.gpsimd.memset(gain_rows[:], 0.0)
-        make_identity(nc, ident[:])
-        load_h(0, 1)
-        load_u(0, 0)
-        load_u(0, 1)
-        for q in range(4):
+        def load_gain(g):
             nc.scalar.dma_start(
-                out=hs_raw[32 * q : 32 * q + 4, :, :].bitcast(I32),
-                in_=h_scales[:, 4 * q : 4 * q + 4, :].rearrange("g q b -> q g b").bitcast(I32),
-            )
-        for g in range(TG):
-            nc.gpsimd.dma_start(
-                out=gain_rows[4 * g : 4 * g + 4, :].rearrange("t (a r) -> t a r", r=4),
-                in_=gain[512 * g : 512 * g + 512].rearrange("(a t r) -> t a r", t=4, r=4),
+                out=gain_rows[PACK * g : PACK * g + PACK, :].rearrange("t (a r) -> t a r", r=4),
+                in_=gain[PASS * g : PASS * g + PASS].rearrange("(a t r) -> t a r", t=PACK, r=4),
             )
 
-        load_u(1, 0)
-        load_h(1, 1)
-        load_u(1, 1)
-        load_v(0)
-        load_h(2, 2)
-        load_v(1)
-        load_v(2)
-        load_v(3)
-        nc.sync.dma_start(out=pw[:], in_=power.partition_broadcast(P))
 
-        def interleave(engine, out, in_):
-            o = out.rearrange("p (c i t) -> p c t i", i=4, t=4)
-            s = in_.rearrange("p t (c i) -> p c t i", i=4)
-            if engine == "v":
-                nc.vector.tensor_copy(out=o, in_=s)
-            else:
-                nc.scalar.copy(out=o, in_=s)
+        def interleave(copy, out, in_):
+            copy(out=out.rearrange("p (c i t) -> p c t i", i=4, t=PACK), in_=in_.rearrange("p t (c i) -> p c t i", i=4))
 
         u_group = {}
-
-        def u_inter(h, k, part, engine):
-            if (h, k) not in u_group:
-                u_group[h, k] = stage.tile([P, 4 * HALF], BF16, align_bytes=64, name="u_grp", bufs=4)
-            interleave(engine, u_group[h, k][:, 1024 * part : 1024 * part + 1024], u_raw[h, k][:, :, 256 * part : 256 * part + 256])
-
-        def u_quant(h, k, part):
-            cols = slice(256 * part, 256 * part + 256)
-            nc.vector.quantize_mx(
-                out=u_codes[:, h, k, cols].bitcast(E4M3), scales=u_scale[:, h, k, cols],
-                in_=u_group[h, k][:, 1024 * part : 1024 * part + 1024],
-            )
-
         v_group = {}
 
-        def v_inter(g, n, engine, part, parts):
-            if (g, n) not in v_group:
-                v_group[g, n] = stage.tile([P, 4 * NH], BF16, align_bytes=64, name="v_grp", bufs=4)
-            w = NH // parts
-            lo = w * part
-            interleave(engine, v_group[g, n][:, 4 * lo : 4 * lo + 4 * w], v_raw[g][:, :, NH * n + lo : NH * n + lo + w])
+        def u_inter(h, k, c, copy):
+            u_group[h, k, c] = stage.tile([P, PACK * QUARTER], BF16, align_bytes=64, name="u_grp", bufs=8)
+            interleave(copy, u_group[h, k, c][:], u_raw[h, k, c][:])
+
+        def u_quant(h, k, c):
+            cols = slice(QUARTER * c, QUARTER * c + QUARTER)
+            nc.vector.quantize_mx(
+                out=u_codes[:, h, k, cols].bitcast(E4M3), scales=u_scale[:, h, k, cols], in_=u_group[h, k, c][:]
+            )
+
+        def v_inter(g, n):
+            v_group[g, n] = stage.tile([P, PACK * NH], BF16, align_bytes=64, name="v_grp", bufs=6)
+            interleave(nc.scalar.copy, v_group[g, n][:], v_raw[g][:, :, NH * n : NH * n + NH])
 
         def v_quant(g, n):
             nc.vector.quantize_mx(
-                out=v_codes[:, g, n, :].bitcast(E4M3), scales=v_scale[:, g, n, :], in_=v_group[g, n][:],
+                out=v_codes[:, g, n, :].bitcast(E4M3), scales=v_scale[:, g, n, :], in_=v_group[g, n][:]
             )
 
         def h_permute(g):
-            for k in range(KG):
+            for k in range(KP):
                 nc.vector.tensor_copy(
-                    out=h_codes[:, k, g, :].bitcast(I32).rearrange("p (t a w) -> p t a w", t=4, w=2),
-                    in_=h_raw[:, k, 1024 * g : 1024 * g + 1024].bitcast(I32).rearrange("p (a t w) -> p t a w", t=4, w=2),
+                    out=h_codes[:, k, g, :].bitcast(I32).rearrange("p (t a w) -> p t a w", t=PACK, w=2),
+                    in_=h_raw[g][:, k, :].bitcast(I32).rearrange("p (a t w) -> p t a w", t=PACK, w=2),
                 )
 
-        def h_scale_permute(k):
-            nc.vector.tensor_copy(
-                out=h_scale[:, k, :, :].rearrange("p g b -> p (g b)").bitcast(I32).rearrange("p (g t a) -> p g t a", g=4, t=4),
-                in_=hs_raw[:, k, :].bitcast(I32).rearrange("p (g a t) -> p g t a", g=4, t=4),
-            )
+        def h_scale_permute(first, groups):
+            for k in range(KP):
+                out = h_scale[:, k, first : first + groups, :].rearrange("p g n -> p (g n)").bitcast(I32)
+                in_ = hs_raw[:, k, PASS * first : PASS * (first + groups)].bitcast(I32)
+                nc.vector.tensor_copy(
+                    out=out.rearrange("p (g t a) -> p g t a", g=groups, t=PACK),
+                    in_=in_.rearrange("p (g a t) -> p g t a", g=groups, t=PACK),
+                )
+
 
         s1_bank = {}
+        g_group = {}
 
         def s1(h, g, b):
-            bank = psum.tile([P, 4, P], F32, name="bank%d" % ((16 * h + 4 * g + b) % 3))
-            s1_bank[h, g, b] = bank
+            s1_bank[h, g, b] = bank((BLOCKS * (TG * h + g) + b) % 3, [P, PACK, P], F32)
             cols = slice(P * b, P * b + P)
-            for t in range(4):
-                for k in range(KG):
+            for t in range(PACK):
+                for k in range(KP):
                     nc.tensor.matmul_mx(
-                        out=bank[:, t, :],
-                        lhsT=h_codes[:, k, g, 256 * t : 256 * t + 256].bitcast(E2M1),
+                        out=s1_bank[h, g, b][:, t, :],
+                        lhsT=h_codes[:, k, g, 2 * P * t : 2 * P * t + 2 * P].bitcast(E2M1),
                         lhsT_scale=h_scale[:, k, g, P * t : P * t + P],
                         rhs=u_codes[:, h, k, cols].bitcast(E4M3),
                         rhs_scale=u_scale[:, h, k, cols],
-                        start=(k == 0), stop=(k == KG - 1),
+                        start=(k == 0),
+                        stop=(k == KP - 1),
                     )
-
-        g_group = {}
 
         def g_copy(h, g, b):
             if b == 0:
-                g_group[h, g] = stage.tile([P, B, P, 4], BF16, align_bytes=64, name="g_grp", bufs=2)
+                g_group[h, g] = stage.tile([P, B, P, PACK], BF16, align_bytes=64, name="g_grp", bufs=2)
+            gains = gain_cols[:, PACK * g : PACK * g + PACK].unsqueeze(1).unsqueeze(1)
             nc.vector.tensor_tensor(
-                out=g_group[h, g][:, :, 32 * b : 32 * b + 32, :],
+                out=g_group[h, g][:, :, SETS * b : SETS * b + SETS, :],
                 in0=s1_bank[h, g, b][:].rearrange("p t (i a) -> p a i t", a=B),
-                in1=gain_cols[:, 4 * g : 4 * g + 4].unsqueeze(1).unsqueeze(1).to_broadcast([P, B, 32, 4]),
+                in1=gains.to_broadcast([P, B, SETS, PACK]),
                 op=MULT,
             )
 
         def g_quant(h, g):
             nc.vector.quantize_mx(
-                out=g_codes[:, h, g, :].bitcast(E5M2), scales=g_scale[:, h, g, :],
+                out=g_codes[:, h, g, :].bitcast(E5M2),
+                scales=g_scale[:, h, g, :],
                 in_=g_group[h, g][:].rearrange("p a i t -> p (a i t)"),
             )
 
+
+        S2_BANKS = {(0, 0): (3, 4, 5, 6), (0, 1): (7, 3, 4, 5), (1, 0): (6, 7, 3, 4), (1, 1): (5, 0, 1, 2)}
         s2_bank = {}
-        BANKS = {(0, 0): (3, 4, 5, 6), (0, 1): (7, 3, 4, 5), (1, 0): (6, 7, 3, 4), (1, 1): (5, 0, 1, 2)}
+        squares = {}
+        total = {}
+        leak_sb = {}
 
         def s2(h, n, a, g):
             if g == 0:
-                s2_bank[h, n, a] = psum.tile([P, NH], F32, name="bank%d" % BANKS[h, n][a])
+                s2_bank[h, n, a] = bank(S2_BANKS[h, n][a], [P, NH], F32)
             cols = slice(P * a, P * a + P)
             nc.tensor.matmul_mx(
                 out=s2_bank[h, n, a][:],
@@ -194,163 +191,150 @@ def tile_interference_alignment_leakage_s9_kernel(tc, u, h_words, h_scales, gain
                 lhsT_scale=g_scale[:, h, g, cols],
                 rhs=v_codes[:, g, n, :].bitcast(E4M3),
                 rhs_scale=v_scale[:, g, n, :],
-                start=(g == 0), stop=(g == TG - 1),
+                start=(g == 0),
+                stop=(g == TG - 1),
             )
 
-        squares = {}
-
-        def f_copy(h, n, a, engine="s"):
-            bank = s2_bank[h, n, a]
-            dst = f_sb[:, h, a, NH * n : NH * n + NH]
-            if engine == "s":
-                nc.scalar.copy(out=dst, in_=bank[:])
-            else:
-                nc.vector.tensor_copy(out=dst, in_=bank[:])
+        def f_copy(h, n, a, copy):
+            tile = f_sb[:, h, a, NH * n : NH * n + NH]
+            copy(out=tile, in_=s2_bank[h, n, a][:])
             rows = out_0[HALF * h : HALF * h + HALF, NH * n : NH * n + NH].rearrange("(i a) n -> i a n", a=B)
-            nc.sync.dma_start(out=rows[:, a, :], in_=dst)
+            nc.sync.dma_start(out=rows[:, a, :], in_=tile)
 
-        def f_square(h, n, a, psum=False, parts=1, part=0):
+        def f_square(h, n, a, cols, from_psum):
             if a == 0:
-                squares[h, n] = stage.tile([P, B, NH], F32, align_bytes=64, name="sq", bufs=2)
-            w = NH // parts
-            lo = w * part
-            src = s2_bank[h, n, a][:, lo : lo + w] if psum else f_sb[:, h, a, NH * n + lo : NH * n + lo + w]
-            nc.scalar.activation(out=squares[h, n][:, a, lo : lo + w], in_=src, func=ACTF.Square)
+                squares[h, n] = stage.tile([P, B, NH], F32, align_bytes=64, name="squares", bufs=2)
+            source = s2_bank[h, n, a][:, cols] if from_psum else f_sb[:, h, a, NH * n : NH * n + NH][:, cols]
+            nc.scalar.activation(out=squares[h, n][:, a, cols], in_=source, func=SQUARE)
 
-        total = {}
-
-        def leak_add(h, n, a, parts=1, part=0):
-            if a == 1 and part == 0:
+        def leak_add(h, n, a, cols):
+            if a == 1:
                 total[h, n] = stage.tile([P, NH], F32, align_bytes=64, name="total", bufs=3)
-            w = NH // parts
-            cols = slice(w * part, w * part + w)
-            nc.vector.tensor_tensor(
-                out=total[h, n][:, cols],
-                in0=squares[h, n][:, 0, cols] if a == 1 else total[h, n][:, cols],
-                in1=squares[h, n][:, a, cols], op=ADD,
-            )
+            so_far = squares[h, n][:, 0, cols] if a == 1 else total[h, n][:, cols]
+            nc.vector.tensor_tensor(out=total[h, n][:, cols], in0=so_far, in1=squares[h, n][:, a, cols], op=ADD)
 
-        def leak_weigh(h, n, parts=1, part=0):
-            w = NH // parts
-            lo = w * part
-            nc.vector.tensor_tensor(
-                out=total[h, n][:, lo : lo + w], in0=total[h, n][:, lo : lo + w], in1=pw[:, NH * n + lo : NH * n + lo + w], op=MULT,
-            )
+        def leak_weigh(h, n, cols):
+            weights = power_sb[:, NH * n : NH * n + NH][:, cols]
+            nc.vector.tensor_tensor(out=total[h, n][:, cols], in0=total[h, n][:, cols], in1=weights, op=MULT)
 
-        leak_sb = {}
-
-        def leak_sum(h, n, parts=1, part=0):
-            if part == 0:
+        def leak_sum(h, n, cols):
+            if cols.start == 0:
                 leak_sb[h, n] = stage.tile([P, P], F32, align_bytes=64, name="leak", bufs=2)
-            w = NH // parts
             nc.vector.tensor_reduce(
-                out=leak_sb[h, n][:, w * part // B : w * (part + 1) // B],
-                in_=total[h, n][:, w * part : w * part + w].rearrange("p (j b) -> p j b", b=B), axis=mybir.AxisListType.X, op=ADD,
+                out=leak_sb[h, n][:, cols.start // B : cols.stop // B],
+                in_=total[h, n][:, cols].rearrange("p (j b) -> p j b", b=B),
+                axis=mybir.AxisListType.X,
+                op=ADD,
             )
-            if part == parts - 1:
+            if cols.stop == NH:
                 nc.sync.dma_start(out=out_1[P * h : P * h + P, P * n : P * n + P], in_=leak_sb[h, n][:])
 
-        todo = {}
 
-        def at(slot, fn, *args):
-            todo.setdefault(slot, []).append((fn, args))
+        make_identity(nc, ident[:])
+        nc.gpsimd.memset(zeros[:], 0.0)
+        nc.vector.memset(gain_rows[:], 0.0)
+        nc.vector.memset(hs_raw[:].rearrange("p k n -> p (k n)").bitcast(I32), 0)
+        nc.vector.memset(one_column[:], 0.0)
+        for g in range(TG):
+            load_gain(g)
+        load_u(0, 0, 0)
+        load_u(0, 1, 0)
+        load_h(0)
+        load_u(0, 0, 1)
+        for q in range(4):
+            load_h_scales(q)
+        load_u(0, 1, 1)
+        load_u(1, 0, 0)
+        load_u(1, 0, 1)
+        load_h(1)
+        load_u(1, 1, 0)
+        load_u(1, 1, 1)
+        load_v(0)
+        load_h(2)
+        load_h(3)
+        load_v(1)
+        load_v(2)
+        load_v(3)
+        nc.sync.dma_start(out=power_sb[:], in_=power.partition_broadcast(P))
 
-        def order():
-            h_scale_permute(0)
-            h_scale_permute(1)
-            h_permute(0)
-            u_inter(0, 0, 0, "v")
-            u_inter(0, 0, 1, "s")
-            u_quant(0, 0, 0)
-            u_inter(0, 1, 0, "v")
-            u_inter(0, 1, 1, "s")
-            gain_ps = psum.tile([P, P], BF16, name="bank7")
-            nc.tensor.transpose(gain_ps[:], gain_rows[:], ident[:])
-            u_quant(0, 1, 0)
-            nc.vector.tensor_copy(out=gain_cols[:], in_=gain_ps[:, 0:16])
+        nc.scalar.activation(out=one_column[:, 0:1], in_=one_column[:, 1:2], func=SQUARE)
+        idle = bank(6, [P, 512], F32)
+        for i in range(12):
+            nc.tensor.matmul(idle[:], lhsT=ident[:], rhs=zeros[:], start=True, stop=True)
 
-            at(0, u_quant, 0, 0, 1)
-            at(0, u_quant, 0, 1, 1)
-            for g in range(1, TG):
-                at(4 * g - 2, h_permute, g)
-            for k in range(KG):
-                for part in range(2):
-                    at(0, u_inter, 1, k, part, "s")
-                    at(6 + 4 * k + part, u_quant, 1, k, part)
+        for k in range(KP):
+            u_inter(0, k, 0, nc.vector.tensor_copy)
+        for k in range(KP):
+            u_quant(0, k, 0)
+        turned = bank(7, [P, P], BF16)
+        nc.tensor.transpose(turned[:], gain_rows[:], ident[:])
+        nc.vector.tensor_copy(out=gain_cols[:], in_=turned[:, 0 : TG * PACK])
+        h_permute(0)
+        h_scale_permute(0, 1)
+        u_inter(0, 0, 1, nc.scalar.copy)
+        h_scale_permute(1, TG - 1)
+
+
+        plan = []
+
+        def at(due, step, *args):
+            plan.append((due, RANK.index(step), len(plan), args))
+
+        RANK = (g_copy, g_quant, u_inter, u_quant, h_permute, v_inter, v_quant, s1, s2, f_copy, f_square, leak_add, leak_weigh, leak_sum)
+        WHOLE = slice(0, NH)
+        ENDS = (slice(0, NH // 2), slice(NH // 2, NH))
+        by_scalar, by_vector = nc.scalar.copy, nc.vector.tensor_copy
+
+        at(0, u_inter, 0, 1, 1, by_vector)
+        for k in range(KP):
+            at(0, u_quant, 0, k, 1)
+            for c in range(2):
+                at(1, u_inter, 1, k, c, by_scalar)
+                at(9 + 2 * (2 * k + c), u_quant, 1, k, c)
+        for g in range(1, TG):
+            at(BLOCKS * g - 3, h_permute, g)
+        for h in range(2):
             for g in range(TG):
-                at(1, v_inter, g, 0, "s", 0, 1)
-                at(9 + 3 * g, v_quant, g, 0)
-            for g in range(3):
-                at(12, v_inter, g, 1, "s", 0, 1)
-                at(17 + 3 * g, v_quant, g, 1)
-            at(18, v_inter, 3, 1, "v", 0, 2)
-            at(20, v_inter, 3, 1, "v", 1, 2)
-            at(22, v_quant, 3, 1)
-            for a in range(B):
-                for g in range(TG):
-                    at(3 * g + 11 + a, s2, 0, 0, a, g)
-                    at(24 + a, s2, 0, 1, a, g)
-                    at(28 + a if g < 3 else 34, s2, 1, 0, a, g)
-                    at(39 + a, s2, 1, 1, a, g)
-            for a in range(B):
-                at(21 + a, f_copy, 0, 0, a)
-                at(24 + a, f_square, 0, 0, a)
-                at(25 + a, f_copy, 0, 1, a, "s")
-                at(27 + a, f_square, 0, 1, a)
-                at(36 + a, f_copy, 1, 0, a, "s" if a % 2 else "s")
-                at(36 + a, f_square, 1, 0, a)
-            for i in range(3):
-                at(28 + i, leak_add, 0, 0, i + 1)
-                at(33 + i, leak_add, 0, 1, i + 1)
-            at(31, leak_weigh, 0, 0)
-            at(32, leak_sum, 0, 0)
-            at(36, leak_weigh, 0, 1)
-            at(37, leak_sum, 0, 1)
-            at(40, f_copy, 1, 1, 0, "v")
-            at(40, f_square, 1, 1, 0)
-            at(40, leak_add, 1, 0, 1)
-            at(41, f_copy, 1, 1, 1, "v")
-            at(41, f_square, 1, 1, 1)
-            at(42, leak_add, 1, 0, 2)
-            at(42, leak_add, 1, 0, 3)
-            at(43, f_copy, 1, 1, 2, "v")
-            at(43, leak_weigh, 1, 0)
-            at(43, f_square, 1, 1, 2)
-            at(44, leak_add, 1, 1, 1)
-            at(44, leak_sum, 1, 0)
-            at(44, leak_add, 1, 1, 2)
-            for part in range(2):
-                at(44, f_square, 1, 1, 3, True, 2, part)
-            at(44, f_copy, 1, 1, 3, "s")
-            for part in range(2):
-                at(44, leak_add, 1, 1, 3, 2, part)
-            for part in range(2):
-                at(45, leak_weigh, 1, 1, 2, part)
-            for part in range(2):
-                at(46, leak_sum, 1, 1, 2, part)
+                first = BLOCKS * (TG * h + g)
+                at(first + 6.5, g_quant, h, g)
+                for b in range(BLOCKS):
+                    n = first + b
+                    at(n, g_copy, h, g, b)
+                    at(max(n - 2, 1) if n > 1 else -1, s1, h, g, b)
+        for n in range(2):
+            for g in range(TG):
+                at(6, v_inter, g, n)
+        for g in range(TG):
+            at(8 + 4 * g, v_quant, g, 0)
+            at(25 + 1.5 * g, v_quant, g, 1)
+        for a in range(B):
+            for g in range(TG):
+                at(8 + 5 * g + a, s2, 0, 0, a, g)
+                at(31 + 0.5 * a, s2, 0, 1, a, g)
+                at(37 + a, s2, 1, 0, a, g)
+                at(44 + 1.5 * a, s2, 1, 1, a, g)
+            at(26.5 + a, f_copy, 0, 0, a, by_scalar)
+            at(27.5 + a, f_square, 0, 0, a, WHOLE, False)
+            at(31.5 + 0.5 * a, f_copy, 0, 1, a, by_scalar)
+            at(32 + 0.5 * a, f_square, 0, 1, a, WHOLE, False)
+            at(38 + a, f_copy, 1, 0, a, by_scalar)
+            at(39.5 + a, f_square, 1, 0, a, WHOLE, False)
+        for a in range(B - 1):
+            at(44 + 1.5 * a, f_copy, 1, 1, a, by_vector if a else by_scalar)
+            at(45 + 1.5 * a, f_square, 1, 1, a, WHOLE, False)
+        for h, n, due, step in ((0, 0, 33, 2), (0, 1, 39, 1), (1, 0, 43.5, 1.5)):
+            for a in range(1, B):
+                at(due + step * (a - 1), leak_add, h, n, a, WHOLE)
+            at(due + 3 * step, leak_weigh, h, n, WHOLE)
+            at(due + 4 * step, leak_sum, h, n, WHOLE)
+        for a in (1, 2):
+            at(45.5 + 1.5 * a, leak_add, 1, 1, a, WHOLE)
+        for cols in ENDS:
+            at(49, f_square, 1, 1, 3, cols, True)
+            at(51, leak_add, 1, 1, 3, cols)
+            at(52, leak_weigh, 1, 1, cols)
+            at(53, leak_sum, 1, 1, cols)
+        at(50, f_copy, 1, 1, 3, by_scalar)
 
-            def name(s):
-                return s // 16, (s // 4) % 4, s % 4
-
-            s1(*name(0))
-            s1(*name(1))
-            for s in range(max(todo) + 1):
-                if s < 32:
-                    g_copy(*name(s))
-                if 4 <= s <= 32 and s % 4 == 0:
-                    g_quant(*name(s - 1)[:2])
-                if s < 32:
-                    for fn, args in todo.get(s, ()):
-                        if fn is not s2:
-                            fn(*args)
-                    if s + 2 < 32:
-                        s1(*name(s + 2))
-                    for fn, args in todo.get(s, ()):
-                        if fn is s2:
-                            fn(*args)
-                else:
-                    for fn, args in todo.get(s, ()):
-                        fn(*args)
-
-        with tc.manual_schedule():
-            order()
+        for due, rank, turn, args in sorted(plan, key=lambda entry: entry[:3]):
+            RANK[rank](*args)

from contextlib import ExitStack

import concourse.mybir as mybir
from concourse.masks import make_identity

R, M, T, N = 1024, 1024, 2048, 1024
B = 4

FLOPS = 2 * R * M * T + 2 * M * T * N + 4 * M * N

F32 = mybir.dt.float32
BF16 = mybir.dt.bfloat16
I32 = mybir.dt.int32
U32 = mybir.dt.uint32
U8 = mybir.dt.uint8
E4M3 = mybir.dt.float8_e4m3fn_x4
E5M2 = mybir.dt.float8_e5m2_x4
E2M1 = mybir.dt.float4_e2m1fn_x4
ADD = mybir.AluOpType.add
MULT = mybir.AluOpType.mult
SQUARE = mybir.ActivationFunctionType.Square

P = 128
PACK = 4
PASS = P * PACK
KP = R // PASS
TG = T // PASS
HALF = M // 2
BLOCKS = HALF // P
SETS = P // B
NH = N // 2
QUARTER = 256


def tile_interference_alignment_leakage_s9_kernel(tc, u, h_words, h_scales, gain, v, power, out_0, out_1):
    nc = tc.nc
    with ExitStack() as ctx:
        keep = ctx.enter_context(tc.tile_pool(name="keep", bufs=1))
        stage = ctx.enter_context(tc.tile_pool(name="stage", bufs=2))
        psum = ctx.enter_context(tc.psum_pool(name="psum", bufs=1))
        ctx.enter_context(tc.manual_schedule())

        def sbuf(shape, dtype, name):
            return keep.tile(shape, dtype, align_bytes=64, name=name)

        def bank(index, shape, dtype):
            return psum.tile(shape, dtype, name="bank%d" % index)

        u_raw = {(h, k, c): sbuf([P, PACK, QUARTER], BF16, "u_raw%d%d%d" % (h, k, c)) for h in range(2) for k in range(KP) for c in range(2)}
        u_codes = sbuf([P, 2, KP, HALF], U32, "u_codes")
        u_scale = sbuf([P, 2, KP, HALF], U8, "u_scale")
        h_raw = [sbuf([P, KP, 2 * PASS], U8, "h_raw%d" % g) for g in range(TG)]
        h_codes = sbuf([P, KP, TG, 2 * PASS], U8, "h_codes")
        hs_raw = sbuf([P, KP, T], U8, "hs_raw")
        h_scale = sbuf([P, KP, TG, PASS], U8, "h_scale")
        v_raw = [sbuf([P, PACK, N], BF16, "v_raw%d" % g) for g in range(TG)]
        v_codes = sbuf([P, TG, 2, NH], U32, "v_codes")
        v_scale = sbuf([P, TG, 2, NH], U8, "v_scale")
        g_codes = sbuf([P, 2, TG, HALF], U32, "g_codes")
        g_scale = sbuf([P, 2, TG, HALF], U8, "g_scale")
        f_sb = sbuf([P, 2, B, N], F32, "f_sb")
        power_sb = sbuf([P, N], BF16, "power_sb")
        gain_rows = sbuf([P, P], BF16, "gain_rows")
        gain_cols = sbuf([P, TG * PACK], F32, "gain_cols")
        ident = sbuf([P, P], BF16, "ident")
        zeros = sbuf([P, 512], BF16, "zeros")
        one_column = sbuf([P, 2], F32, "one_column")


        def load_u(h, k, c):
            lo = HALF * h + QUARTER * c
            nc.sync.dma_start(
                out=u_raw[h, k, c][:],
                in_=u[PASS * k : PASS * k + PASS, lo : lo + QUARTER].rearrange("(p t) w -> p t w", t=PACK),
            )

        def load_h(g):
            words = h_words.rearrange("k p b -> p k b")[:, :, 2 * PASS * g : 2 * PASS * g + 2 * PASS]
            nc.sync.dma_start(out=h_raw[g][:].bitcast(I32), in_=words.bitcast(I32))

        def load_h_scales(q):
            nc.sync.dma_start(
                out=hs_raw[32 * q : 32 * q + 4, :, :].bitcast(I32),
                in_=h_scales[:, 4 * q : 4 * q + 4, :].rearrange("k q n -> q k n").bitcast(I32),
            )

        def load_v(g):
            rows = v[PASS * g : PASS * g + PASS, :].rearrange("(a t r) n -> r a t n", t=PACK, r=4)
            for r in range(4):
                nc.sync.dma_start(out=v_raw[g][r:P:4, :, :], in_=rows[r])

        def load_gain(g):
            nc.scalar.dma_start(
                out=gain_rows[PACK * g : PACK * g + PACK, :].rearrange("t (a r) -> t a r", r=4),
                in_=gain[PASS * g : PASS * g + PASS].rearrange("(a t r) -> t a r", t=PACK, r=4),
            )


        def interleave(copy, out, in_):
            copy(out=out.rearrange("p (c i t) -> p c t i", i=4, t=PACK), in_=in_.rearrange("p t (c i) -> p c t i", i=4))

        u_group = {}
        v_group = {}

        def u_inter(h, k, c, copy):
            u_group[h, k, c] = stage.tile([P, PACK * QUARTER], BF16, align_bytes=64, name="u_grp", bufs=8)
            interleave(copy, u_group[h, k, c][:], u_raw[h, k, c][:])

        def u_quant(h, k, c):
            cols = slice(QUARTER * c, QUARTER * c + QUARTER)
            nc.vector.quantize_mx(
                out=u_codes[:, h, k, cols].bitcast(E4M3), scales=u_scale[:, h, k, cols], in_=u_group[h, k, c][:]
            )

        def v_inter(g, n):
            v_group[g, n] = stage.tile([P, PACK * NH], BF16, align_bytes=64, name="v_grp", bufs=6)
            interleave(nc.scalar.copy, v_group[g, n][:], v_raw[g][:, :, NH * n : NH * n + NH])

        def v_quant(g, n):
            nc.vector.quantize_mx(
                out=v_codes[:, g, n, :].bitcast(E4M3), scales=v_scale[:, g, n, :], in_=v_group[g, n][:]
            )

        def h_permute(g):
            for k in range(KP):
                nc.vector.tensor_copy(
                    out=h_codes[:, k, g, :].bitcast(I32).rearrange("p (t a w) -> p t a w", t=PACK, w=2),
                    in_=h_raw[g][:, k, :].bitcast(I32).rearrange("p (a t w) -> p t a w", t=PACK, w=2),
                )

        def h_scale_permute(first, groups):
            for k in range(KP):
                out = h_scale[:, k, first : first + groups, :].rearrange("p g n -> p (g n)").bitcast(I32)
                in_ = hs_raw[:, k, PASS * first : PASS * (first + groups)].bitcast(I32)
                nc.vector.tensor_copy(
                    out=out.rearrange("p (g t a) -> p g t a", g=groups, t=PACK),
                    in_=in_.rearrange("p (g a t) -> p g t a", g=groups, t=PACK),
                )


        s1_bank = {}
        g_group = {}

        def s1(h, g, b):
            s1_bank[h, g, b] = bank((BLOCKS * (TG * h + g) + b) % 3, [P, PACK, P], F32)
            cols = slice(P * b, P * b + P)
            for t in range(PACK):
                for k in range(KP):
                    nc.tensor.matmul_mx(
                        out=s1_bank[h, g, b][:, t, :],
                        lhsT=h_codes[:, k, g, 2 * P * t : 2 * P * t + 2 * P].bitcast(E2M1),
                        lhsT_scale=h_scale[:, k, g, P * t : P * t + P],
                        rhs=u_codes[:, h, k, cols].bitcast(E4M3),
                        rhs_scale=u_scale[:, h, k, cols],
                        start=(k == 0),
                        stop=(k == KP - 1),
                    )

        def g_copy(h, g, b):
            if b == 0:
                g_group[h, g] = stage.tile([P, B, P, PACK], BF16, align_bytes=64, name="g_grp", bufs=2)
            gains = gain_cols[:, PACK * g : PACK * g + PACK].unsqueeze(1).unsqueeze(1)
            nc.vector.tensor_tensor(
                out=g_group[h, g][:, :, SETS * b : SETS * b + SETS, :],
                in0=s1_bank[h, g, b][:].rearrange("p t (i a) -> p a i t", a=B),
                in1=gains.to_broadcast([P, B, SETS, PACK]),
                op=MULT,
            )

        def g_quant(h, g):
            nc.vector.quantize_mx(
                out=g_codes[:, h, g, :].bitcast(E5M2),
                scales=g_scale[:, h, g, :],
                in_=g_group[h, g][:].rearrange("p a i t -> p (a i t)"),
            )


        S2_BANKS = {(0, 0): (3, 4, 5, 6), (0, 1): (7, 3, 4, 5), (1, 0): (6, 7, 3, 4), (1, 1): (5, 0, 1, 2)}
        s2_bank = {}
        squares = {}
        total = {}
        leak_sb = {}

        def s2(h, n, a, g):
            if g == 0:
                s2_bank[h, n, a] = bank(S2_BANKS[h, n][a], [P, NH], F32)
            cols = slice(P * a, P * a + P)
            nc.tensor.matmul_mx(
                out=s2_bank[h, n, a][:],
                lhsT=g_codes[:, h, g, cols].bitcast(E5M2),
                lhsT_scale=g_scale[:, h, g, cols],
                rhs=v_codes[:, g, n, :].bitcast(E4M3),
                rhs_scale=v_scale[:, g, n, :],
                start=(g == 0),
                stop=(g == TG - 1),
            )

        def f_copy(h, n, a, copy):
            tile = f_sb[:, h, a, NH * n : NH * n + NH]
            copy(out=tile, in_=s2_bank[h, n, a][:])
            rows = out_0[HALF * h : HALF * h + HALF, NH * n : NH * n + NH].rearrange("(i a) n -> i a n", a=B)
            nc.sync.dma_start(out=rows[:, a, :], in_=tile)

        def f_square(h, n, a, cols, from_psum):
            if a == 0:
                squares[h, n] = stage.tile([P, B, NH], F32, align_bytes=64, name="squares", bufs=2)
            source = s2_bank[h, n, a][:, cols] if from_psum else f_sb[:, h, a, NH * n : NH * n + NH][:, cols]
            nc.scalar.activation(out=squares[h, n][:, a, cols], in_=source, func=SQUARE)

        def leak_add(h, n, a, cols):
            if a == 1:
                total[h, n] = stage.tile([P, NH], F32, align_bytes=64, name="total", bufs=3)
            so_far = squares[h, n][:, 0, cols] if a == 1 else total[h, n][:, cols]
            nc.vector.tensor_tensor(out=total[h, n][:, cols], in0=so_far, in1=squares[h, n][:, a, cols], op=ADD)

        def leak_weigh(h, n, cols):
            weights = power_sb[:, NH * n : NH * n + NH][:, cols]
            nc.vector.tensor_tensor(out=total[h, n][:, cols], in0=total[h, n][:, cols], in1=weights, op=MULT)

        def leak_sum(h, n, cols):
            if cols.start == 0:
                leak_sb[h, n] = stage.tile([P, P], F32, align_bytes=64, name="leak", bufs=2)
            nc.vector.tensor_reduce(
                out=leak_sb[h, n][:, cols.start // B : cols.stop // B],
                in_=total[h, n][:, cols].rearrange("p (j b) -> p j b", b=B),
                axis=mybir.AxisListType.X,
                op=ADD,
            )
            if cols.stop == NH:
                nc.sync.dma_start(out=out_1[P * h : P * h + P, P * n : P * n + P], in_=leak_sb[h, n][:])


        make_identity(nc, ident[:])
        nc.gpsimd.memset(zeros[:], 0.0)
        nc.vector.memset(gain_rows[:], 0.0)
        nc.vector.memset(hs_raw[:].rearrange("p k n -> p (k n)").bitcast(I32), 0)
        nc.vector.memset(one_column[:], 0.0)
        for g in range(TG):
            load_gain(g)
        load_u(0, 0, 0)
        load_u(0, 1, 0)
        load_h(0)
        load_u(0, 0, 1)
        for q in range(4):
            load_h_scales(q)
        load_u(0, 1, 1)
        load_u(1, 0, 0)
        load_u(1, 0, 1)
        load_h(1)
        load_u(1, 1, 0)
        load_u(1, 1, 1)
        load_v(0)
        load_h(2)
        load_h(3)
        load_v(1)
        load_v(2)
        load_v(3)
        nc.sync.dma_start(out=power_sb[:], in_=power.partition_broadcast(P))

        nc.scalar.activation(out=one_column[:, 0:1], in_=one_column[:, 1:2], func=SQUARE)
        idle = bank(6, [P, 512], F32)
        for i in range(12):
            nc.tensor.matmul(idle[:], lhsT=ident[:], rhs=zeros[:], start=True, stop=True)

        for k in range(KP):
            u_inter(0, k, 0, nc.vector.tensor_copy)
        for k in range(KP):
            u_quant(0, k, 0)
        turned = bank(7, [P, P], BF16)
        nc.tensor.transpose(turned[:], gain_rows[:], ident[:])
        nc.vector.tensor_copy(out=gain_cols[:], in_=turned[:, 0 : TG * PACK])
        h_permute(0)
        h_scale_permute(0, 1)
        u_inter(0, 0, 1, nc.scalar.copy)
        h_scale_permute(1, TG - 1)


        plan = []

        def at(due, step, *args):
            plan.append((due, RANK.index(step), len(plan), args))

        RANK = (g_copy, g_quant, u_inter, u_quant, h_permute, v_inter, v_quant, s1, s2, f_copy, f_square, leak_add, leak_weigh, leak_sum)
        WHOLE = slice(0, NH)
        ENDS = (slice(0, NH // 2), slice(NH // 2, NH))
        by_scalar, by_vector = nc.scalar.copy, nc.vector.tensor_copy

        at(0, u_inter, 0, 1, 1, by_vector)
        for k in range(KP):
            at(0, u_quant, 0, k, 1)
            for c in range(2):
                at(1, u_inter, 1, k, c, by_scalar)
                at(9 + 2 * (2 * k + c), u_quant, 1, k, c)
        for g in range(1, TG):
            at(BLOCKS * g - 3, h_permute, g)
        for h in range(2):
            for g in range(TG):
                first = BLOCKS * (TG * h + g)
                at(first + 6.5, g_quant, h, g)
                for b in range(BLOCKS):
                    n = first + b
                    at(n, g_copy, h, g, b)
                    at(max(n - 2, 1) if n > 1 else -1, s1, h, g, b)
        for n in range(2):
            for g in range(TG):
                at(6, v_inter, g, n)
        for g in range(TG):
            at(8 + 4 * g, v_quant, g, 0)
            at(25 + 1.5 * g, v_quant, g, 1)
        for a in range(B):
            for g in range(TG):
                at(8 + 5 * g + a, s2, 0, 0, a, g)
                at(31 + 0.5 * a, s2, 0, 1, a, g)
                at(37 + a, s2, 1, 0, a, g)
                at(44 + 1.5 * a, s2, 1, 1, a, g)
            at(26.5 + a, f_copy, 0, 0, a, by_scalar)
            at(27.5 + a, f_square, 0, 0, a, WHOLE, False)
            at(31.5 + 0.5 * a, f_copy, 0, 1, a, by_scalar)
            at(32 + 0.5 * a, f_square, 0, 1, a, WHOLE, False)
            at(38 + a, f_copy, 1, 0, a, by_scalar)
            at(39.5 + a, f_square, 1, 0, a, WHOLE, False)
        for a in range(B - 1):
            at(44 + 1.5 * a, f_copy, 1, 1, a, by_vector if a else by_scalar)
            at(45 + 1.5 * a, f_square, 1, 1, a, WHOLE, False)
        for h, n, due, step in ((0, 0, 33, 2), (0, 1, 39, 1), (1, 0, 43.5, 1.5)):
            for a in range(1, B):
                at(due + step * (a - 1), leak_add, h, n, a, WHOLE)
            at(due + 3 * step, leak_weigh, h, n, WHOLE)
            at(due + 4 * step, leak_sum, h, n, WHOLE)
        for a in (1, 2):
            at(45.5 + 1.5 * a, leak_add, 1, 1, a, WHOLE)
        for cols in ENDS:
            at(49, f_square, 1, 1, 3, cols, True)
            at(51, leak_add, 1, 1, 3, cols)
            at(52, leak_weigh, 1, 1, cols)
            at(53, leak_sum, 1, 1, cols)
        at(50, f_copy, 1, 1, 3, by_scalar)

        for due, rank, turn, args in sorted(plan, key=lambda entry: entry[:3]):
            RANK[rank](*args)
